import numpy as np
import ml_dtypes


def mxq(x, axis, fmt="e4m3"):
    dtype, down = {"e4m3": (ml_dtypes.float8_e4m3fn, 7), "e5m2": (ml_dtypes.float8_e5m2, 14)}[fmt]
    v = np.moveaxis(np.asarray(x, np.float32).astype(ml_dtypes.bfloat16).astype(np.float64), axis, -1)
    blocks = v.reshape(v.shape[:-1] + (-1, 32))
    amax = np.abs(blocks).max(-1, keepdims=True)
    byte = np.maximum(np.where(amax > 0, np.frexp(amax)[1] - 1 + 127, 0) - down, 1)
    scale = np.exp2(byte - 127.0)
    codes = (blocks / scale).astype(np.float32).astype(dtype).astype(np.float64)
    return np.moveaxis((codes * scale).reshape(v.shape), -1, axis)


WIDE = False


def mx_kscale(k, group=512):
    if not WIDE:
        return np.ones(k)
    levels = np.array([18, -18])
    if group != 512:
        return np.exp2(np.random.permutation(np.resize(levels, k // group))).repeat(group)
    if k % 512:
        return np.exp2(np.random.permutation(np.resize(levels, k // 32))).repeat(32)
    a = np.empty((k // 512, 16))
    for p in range(k // 512):
        a[p, :8] = np.random.permutation(np.resize(levels, 8))
        for g in range(8):
            far = levels[np.abs(levels - a[p, g]) >= 10]
            a[p, g + 8] = far[np.random.randint(len(far))]
    return np.exp2(a.ravel()).repeat(32)


def f64(x):
    return np.asarray(x).astype(np.float64)


def bf(x):
    return np.asarray(x, np.float32).astype(ml_dtypes.bfloat16)


def planes(Y):
    r, m = Y.shape
    b = f64(bf(Y)).reshape(r // 32, 32, m)
    amax = np.abs(b).max(1)
    byte = np.clip(np.where(amax > 0, np.frexp(amax)[1] - 1 + 127 - 7, 1), 1, 254)
    codes = (b * np.exp2(127.0 - byte)[:, None, :]).reshape(r, m).astype(np.float32).astype(ml_dtypes.float8_e4m3fn).view(np.uint8)
    words = codes.reshape(r // 512, 128, 4, m).transpose(0, 1, 3, 2)
    return np.ascontiguousarray(words), np.ascontiguousarray(byte.astype(np.uint8).reshape(r // 512, 16, m))


G, D, I, N, J = 4, 128, 128, 512, 128


def sgn(shape):
    return np.random.uniform(0.5, 2.0, shape) * np.where(np.random.standard_normal(shape) < 0, -1.0, 1.0)


def setup_inputs():
    n = np.random.standard_normal
    s_d = mx_kscale(D, 0)
    s_i = mx_kscale(I, 0)
    return {
        "x": (n((G, D, I)) * s_d[:, None]).astype(np.float32),
        "w": (n((D, N)) / np.sqrt(D) / s_d[:, None]).astype(np.float32),
        "ni": (sgn((G, I, 1)) * s_i[:, None]).astype(np.float32),
        "ad": ((np.random.uniform(size=(G, I, J)) < 0.1) * np.random.uniform(0.5, 1.0, (G, I, J)) / 3 / s_i[:, None]).astype(np.float32),
        "bn": (0.5 * n((1, N))).astype(np.float32),
    }


def reference(x, w, ni, ad, bn):
    xq = mxq(f64(x), 1, "e4m3")
    wq = mxq(f64(w), 0, "e4m3")
    z = xq.transpose(0, 2, 1) @ wq
    h = z * f64(ni)
    adq = mxq(f64(ad), 1, "e4m3")
    hq = mxq(h, 1, "e4m3")
    y = adq.transpose(0, 2, 1) @ hq
    out_ = np.maximum(y + f64(bn), 0.0)
    Y = out_.reshape(G * J, N)
    words, scales = planes(Y)
    return Y, words, scales

@@ -1,0 +1,204 @@
+from contextlib import ExitStack
+
+import concourse.mybir as mybir
+
+G, D, I, N, J = 4, 128, 128, 512, 128
+FLOPS = 2 * G * I * N * (D + J)
+
+F32 = mybir.dt.float32
+BF16 = mybir.dt.bfloat16
+I32 = mybir.dt.int32
+U32 = mybir.dt.uint32
+U8 = mybir.dt.uint8
+FP8X4 = mybir.dt.float8_e4m3fn_x4
+ACT = mybir.ActivationFunctionType
+ALU = mybir.AluOpType
+
+P = 128
+R = 32
+PACK = 4
+C = 128
+
+
+def tile_rows_pl_gnn_gcn_kernel(tc, x, w, ni, ad, bn, out_0, out_1, out_2):
+    nc = tc.nc
+
+    def rows(r):
+        return slice(R * r, R * r + R)
+
+    def quantize(codes, scales, src):
+        nc.vector.quantize_mx(out=codes.bitcast(FP8X4), scales=scales, in_=src)
+
+    with ExitStack() as ctx:
+        sb = ctx.enter_context(tc.tile_pool(name="sb", bufs=1))
+        ps = ctx.enter_context(tc.psum_pool(name="ps", bufs=1))
+        ctx.enter_context(tc.manual_schedule())
+
+        x_raw = sb.tile([P, G, PACK, I], F32, name="x_raw", align_bytes=64)
+        w_raw = sb.tile([P, PACK, C], F32, name="w_raw", align_bytes=64)
+        ad_raw = sb.tile([P, PACK, J], F32, name="ad_raw", align_bytes=64)
+        ni_sb = sb.tile([P, PACK], F32, name="ni_sb", align_bytes=64)
+        bn_rows = sb.tile([P, C], F32, name="bn_rows", align_bytes=64)
+        bn_cols = sb.tile([P, C], F32, name="bn_cols", align_bytes=64)
+
+        x_bf = sb.tile([P, PACK, G, R, PACK], BF16, name="x_bf", align_bytes=64)
+        w_bf = sb.tile([P, C, PACK], BF16, name="w_bf", align_bytes=64)
+        ad_bf = sb.tile([P, PACK, R, PACK], BF16, name="ad_bf", align_bytes=64)
+        h_bf = sb.tile([P, 4, 4, R, PACK], BF16, name="h_bf", align_bytes=64)
+
+        x_codes = sb.tile([P, PACK, C], U32, name="x_codes", align_bytes=64)
+        x_scales = sb.tile([P, PACK, C], U8, name="x_scales", align_bytes=64)
+        w_codes = sb.tile([P, C], U32, name="w_codes", align_bytes=64)
+        w_scales = sb.tile([P, C], U8, name="w_scales", align_bytes=64)
+        ad_codes = sb.tile([P, J], U32, name="ad_codes", align_bytes=64)
+        ad_scales = sb.tile([P, J], U8, name="ad_scales", align_bytes=64)
+        h_codes = sb.tile([P, 4, C], U32, name="h_codes", align_bytes=64)
+        h_scales = sb.tile([P, 4, C], U8, name="h_scales", align_bytes=64)
+        y_codes = sb.tile([P, G, C], U32, name="y_codes", align_bytes=64)
+        y_scales = sb.tile([P, G, C], U8, name="y_scales", align_bytes=64)
+
+        y_t = [sb.tile([P, PACK, 4, R], F32, name="y_t%d" % g, align_bytes=64) for g in range(G)]
+        y_f = [sb.tile([P, PACK, C], F32, name="y_f%d" % g, align_bytes=64) for g in range(G)]
+        y_bf = [sb.tile([P, C, PACK], BF16, name="y_bf%d" % g, align_bytes=64) for g in range(G)]
+
+        bank_a = [ps.tile([P, 4, C], F32, name="bank_a%d" % r) for r in range(4)]
+        bank_b = [ps.tile([P, 4, C], F32, name="bank_b%d" % r) for r in range(4)]
+
+        nc.gpsimd.memset(bn_rows[:], 0.0)
+
+        queue = [nc.sync, nc.sync, nc.scalar, nc.scalar]
+        for r in (0, 2, 1, 3):
+            queue[r].dma_start(
+                out=w_raw[rows(r)],
+                in_=w[:, C * r : C * r + C].rearrange("(p j) n -> p j n", j=PACK),
+            )
+        for r in (0, 2, 1, 3):
+            queue[r].dma_start(
+                out=x_raw[rows(r)].rearrange("p g j i -> p g (j i)"),
+                in_=x.rearrange("g (p j) i -> p g (j i)", j=PACK),
+            )
+        nc.sync.dma_start(
+            out=ad_raw[:].rearrange("p t j -> p (t j)"),
+            in_=ad.rearrange("g (p t) j -> (g p) (t j)", t=PACK),
+        )
+        nc.sync.dma_start(out=ni_sb[:], in_=ni.rearrange("g (p t) o -> (g p) (t o)", t=PACK))
+        nc.sync.dma_start(out=bn_rows[0:P:R, :], in_=bn.rearrange("o (a n) -> (o a) n", a=4))
+
+        nc.vector.tensor_copy(
+            out=w_bf[:].rearrange("p (c i) j -> p c j i", i=4),
+            in_=w_raw[:].rearrange("p j (c i) -> p c j i", i=4),
+        )
+        x_out = x_bf[:].rearrange("p t g q j -> p g q j t")
+        x_in = x_raw[:].rearrange("p g j (q t) -> p g q j t", t=PACK)
+        nc.vector.tensor_copy(out=x_out[:, 0:2], in_=x_in[:, 0:2])
+        nc.scalar.copy(out=x_out[:, 3], in_=x_in[:, 3])
+        nc.vector.tensor_copy(out=x_out[:, 2], in_=x_in[:, 2])
+        quantize(w_codes[:], w_scales[:], w_bf[:].rearrange("p c j -> p (c j)"))
+        nc.scalar.copy(
+            out=ad_bf[:].rearrange("p u e t -> p e t u"),
+            in_=ad_raw[:].rearrange("p t (e u) -> p e t u", u=PACK),
+        )
+        for t in range(PACK):
+            quantize(x_codes[:, t, :], x_scales[:, t, :], x_bf[:, t].rearrange("p g q j -> p (g q j)"))
+            for r in range(4):
+                nc.tensor.matmul_mx(
+                    out=bank_a[r][:, t, :],
+                    lhsT=x_codes[rows(r), t, :].bitcast(FP8X4),
+                    lhsT_scale=x_scales[rows(r), t, :],
+                    rhs=w_codes[rows(r), :].bitcast(FP8X4),
+                    rhs_scale=w_scales[rows(r), :],
+                    start=True,
+                    stop=True,
+                )
+        quantize(ad_codes[:], ad_scales[:], ad_bf[:].rearrange("p u e t -> p (u e t)"))
+        nc.vector.transpose(bn_cols[:], bn_rows[:])
+
+        for t in range(PACK):
+            nc.scalar.activation(
+                out=h_bf[:, :, 3, :, t],
+                in_=bank_a[3][:, t, :].rearrange("p (k c) -> p k c", k=4),
+                func=ACT.Copy,
+                scale=ni_sb[:, t : t + 1],
+            )
+        for a in range(3):
+            nc.vector.tensor_tensor(
+                out=h_bf[:, :, a],
+                in0=bank_a[a][:].rearrange("p t (k c) -> p k c t", k=4),
+                in1=ni_sb[:].unsqueeze(1).unsqueeze(1).to_broadcast([P, 4, R, PACK]),
+                op=ALU.mult,
+            )
+
+        def y_bank(g, k):
+            return bank_b[g][:, k, :] if k < 2 else bank_a[g][:, k, :]
+
+        for half in range(2):
+            ks = slice(2 * half, 2 * half + 2)
+            quantize(
+                h_codes[:, ks].rearrange("p k c -> p (k c)"),
+                h_scales[:, ks].rearrange("p k c -> p (k c)"),
+                h_bf[:, ks].rearrange("p k a c t -> p (k a c t)"),
+            )
+            for k in (2 * half, 2 * half + 1):
+                for g in range(G):
+                    nc.tensor.matmul_mx(
+                        out=y_bank(g, k),
+                        lhsT=h_codes[rows(g), k, :].bitcast(FP8X4),
+                        lhsT_scale=h_scales[rows(g), k, :],
+                        rhs=ad_codes[rows(g), :].bitcast(FP8X4),
+                        rhs_scale=ad_scales[rows(g), :],
+                        start=True,
+                        stop=True,
+                    )
+
+        def relu(g, k, on_vector):
+            src = y_bank(g, k).rearrange("p (u e) -> p u e", u=PACK)
+            bias = bn_cols[:, R * k : R * k + 1]
+            if on_vector:
+                nc.vector.tensor_scalar(
+                    out=y_t[g][:, :, k, :], in0=src, scalar1=bias, scalar2=0.0, op0=ALU.add, op1=ALU.max
+                )
+            else:
+                nc.scalar.activation(out=y_t[g][:, :, k, :], in_=src, func=ACT.Relu, bias=bias)
+
+        out_rows = out_0.rearrange("(g e u) (a n) -> g a e u n", g=G, u=PACK, a=4)
+
+        def turn_and_store(g):
+            nc.vector.transpose(
+                y_f[g][:].rearrange("p u n -> p (u n)"), y_t[g][:].rearrange("p u k e -> p (u k e)")
+            )
+            for a in (0, 2, 1, 3):
+                nc.sync.dma_start(out=out_rows[g, a], in_=y_f[g][rows(a)])
+
+        def round_y(g, on_vector):
+            dst = y_bf[g][:].rearrange("p (c i) u -> p c u i", i=4)
+            src = y_f[g][:].rearrange("p u (c i) -> p c u i", i=4)
+            if on_vector:
+                nc.vector.tensor_copy(out=dst, in_=src)
+            else:
+                nc.scalar.copy(out=dst, in_=src)
+
+        def quantize_y(g):
+            quantize(y_codes[:, g, :], y_scales[:, g, :], y_bf[g][:].rearrange("p n u -> p (n u)"))
+
+        for g in range(G):
+            for k in range(4):
+                relu(g, k, g == 0 and k >= 2)
+        turn_and_store(0)
+        turn_and_store(1)
+        round_y(0, True)
+        turn_and_store(2)
+        round_y(1, False)
+        quantize_y(0)
+        turn_and_store(3)
+        round_y(2, False)
+        quantize_y(1)
+        round_y(3, True)
+        quantize_y(2)
+        quantize_y(3)
+
+        words = out_1.rearrange("s p n u -> (s p) (n u)").bitcast(I32).rearrange("(g e) (a n) -> a e g n", g=G, a=4)
+        scale_rows = out_2.rearrange("s f n -> (s f) n").bitcast(I32).rearrange("(g f) (a n) -> a f g n", g=G, a=4)
+        for a in (0, 2, 1, 3):
+            queue[a].dma_start(out=words[a], in_=y_codes[rows(a)].bitcast(I32))
+        for a in (0, 2, 1, 3):
+            queue[a].dma_start(out=scale_rows[a], in_=y_scales[R * a : R * a + 4].bitcast(I32))

@@ -18,6 +18,10 @@ P = 128
 R = 32
 PACK = 4
 C = 128
+H = 256
+SPLIT = 160
+U = 96
+XCUT = 8
 
 
 def tile_rows_pl_gnn_gcn_kernel(tc, x, w, ni, ad, bn, out_0, out_1, out_2):
@@ -34,171 +38,168 @@ def tile_rows_pl_gnn_gcn_kernel(tc, x, w, ni, ad, bn, out_0, out_1, out_2):
         ps = ctx.enter_context(tc.psum_pool(name="ps", bufs=1))
         ctx.enter_context(tc.manual_schedule())
 
-        x_raw = sb.tile([P, G, PACK, I], F32, name="x_raw", align_bytes=64)
-        w_raw = sb.tile([P, PACK, C], F32, name="w_raw", align_bytes=64)
+        x_raw = [sb.tile([P, 2, PACK, I], F32, name="x_raw%d" % m, align_bytes=64) for m in range(2)]
+        w_raw = sb.tile([P, PACK, 2, C], F32, name="w_raw", align_bytes=64)
         ad_raw = sb.tile([P, PACK, J], F32, name="ad_raw", align_bytes=64)
         ni_sb = sb.tile([P, PACK], F32, name="ni_sb", align_bytes=64)
-        bn_rows = sb.tile([P, C], F32, name="bn_rows", align_bytes=64)
-        bn_cols = sb.tile([P, C], F32, name="bn_cols", align_bytes=64)
+        bn_few = sb.tile([P, N], F32, name="bn_few", align_bytes=64)
+        bn_all = sb.tile([P, N], F32, name="bn_all", align_bytes=64)
+        warm_in = sb.tile([P, 8], F32, name="warm_in", align_bytes=64)
 
         x_bf = sb.tile([P, PACK, G, R, PACK], BF16, name="x_bf", align_bytes=64)
-        w_bf = sb.tile([P, C, PACK], BF16, name="w_bf", align_bytes=64)
-        ad_bf = sb.tile([P, PACK, R, PACK], BF16, name="ad_bf", align_bytes=64)
-        h_bf = sb.tile([P, 4, 4, R, PACK], BF16, name="h_bf", align_bytes=64)
+        w_bf = sb.tile([P, 2, C, PACK], BF16, name="w_bf", align_bytes=64)
+        ad_bf = sb.tile([P, J, PACK], BF16, name="ad_bf", align_bytes=64)
+        h_bf = sb.tile([P, 4, C, PACK], BF16, name="h_bf", align_bytes=64)
 
         x_codes = sb.tile([P, PACK, C], U32, name="x_codes", align_bytes=64)
         x_scales = sb.tile([P, PACK, C], U8, name="x_scales", align_bytes=64)
-        w_codes = sb.tile([P, C], U32, name="w_codes", align_bytes=64)
-        w_scales = sb.tile([P, C], U8, name="w_scales", align_bytes=64)
+        w_codes = sb.tile([P, 2, C], U32, name="w_codes", align_bytes=64)
+        w_scales = sb.tile([P, 2, C], U8, name="w_scales", align_bytes=64)
         ad_codes = sb.tile([P, J], U32, name="ad_codes", align_bytes=64)
         ad_scales = sb.tile([P, J], U8, name="ad_scales", align_bytes=64)
         h_codes = sb.tile([P, 4, C], U32, name="h_codes", align_bytes=64)
         h_scales = sb.tile([P, 4, C], U8, name="h_scales", align_bytes=64)
-        y_codes = sb.tile([P, G, C], U32, name="y_codes", align_bytes=64)
-        y_scales = sb.tile([P, G, C], U8, name="y_scales", align_bytes=64)
+        y_codes = sb.tile([P, N], U32, name="y_codes", align_bytes=64)
+        y_scales = sb.tile([P, N], U8, name="y_scales", align_bytes=64)
 
-        y_t = [sb.tile([P, PACK, 4, R], F32, name="y_t%d" % g, align_bytes=64) for g in range(G)]
-        y_f = [sb.tile([P, PACK, C], F32, name="y_f%d" % g, align_bytes=64) for g in range(G)]
-        y_bf = [sb.tile([P, C, PACK], BF16, name="y_bf%d" % g, align_bytes=64) for g in range(G)]
+        sums = [[sb.tile([P, H], F32, name="sums%d_%d" % (h, g), align_bytes=64) for g in range(G)] for h in range(2)]
+        y_f = [sb.tile([P, N], F32, name="y_f%d" % g, align_bytes=64) for g in range(G)]
+        grouped = [sb.tile([P, PACK, H], F32, name="grouped%d" % h, align_bytes=64) for h in range(2)]
+        y_bf = [sb.tile([P, H, PACK], BF16, name="y_bf%d" % h, align_bytes=64) for h in range(2)]
 
         bank_a = [ps.tile([P, 4, C], F32, name="bank_a%d" % r) for r in range(4)]
         bank_b = [ps.tile([P, 4, C], F32, name="bank_b%d" % r) for r in range(4)]
 
-        nc.gpsimd.memset(bn_rows[:], 0.0)
+        nc.gpsimd.memset(warm_in[:], 0.0)
+
+        nc.vector.memset(w_raw[rows(1)].bitcast(I32), 0)
+        nc.vector.memset(x_raw[0][rows(1)].bitcast(I32), 0)
+        nc.gpsimd.memset(x_raw[1][rows(1)].bitcast(I32), 0)
 
         queue = [nc.sync, nc.sync, nc.scalar, nc.scalar]
-        for r in (0, 2, 1, 3):
-            queue[r].dma_start(
-                out=w_raw[rows(r)],
-                in_=w[:, C * r : C * r + C].rearrange("(p j) n -> p j n", j=PACK),
-            )
-        for r in (0, 2, 1, 3):
-            queue[r].dma_start(
-                out=x_raw[rows(r)].rearrange("p g j i -> p g (j i)"),
-                in_=x.rearrange("g (p j) i -> p g (j i)", j=PACK),
-            )
+        w_rows = w.rearrange("(p j) (s b n) -> b p (j s) n", j=PACK, s=2, b=2)
+        x_rows = x.rearrange("(m g) (p j) i -> m p g (j i)", m=2, j=PACK)
+        for b in range(2):
+            queue[2 * b].dma_start(out=w_raw[rows(2 * b)].rearrange("p j s n -> p (j s) n"), in_=w_rows[b])
+        for m in range(2):
+            for b in range(2):
+                queue[2 * b].dma_start(out=x_raw[m][rows(2 * b)].rearrange("p g j i -> p g (j i)"), in_=x_rows[m])
         nc.sync.dma_start(
             out=ad_raw[:].rearrange("p t j -> p (t j)"),
             in_=ad.rearrange("g (p t) j -> (g p) (t j)", t=PACK),
         )
-        nc.sync.dma_start(out=ni_sb[:], in_=ni.rearrange("g (p t) o -> (g p) (t o)", t=PACK))
-        nc.sync.dma_start(out=bn_rows[0:P:R, :], in_=bn.rearrange("o (a n) -> (o a) n", a=4))
+        nc.scalar.dma_start(out=ni_sb[:], in_=ni.rearrange("g (p t) o -> (g p) (t o)", t=PACK))
+        warm = sb.tile([P, 8], F32, name="warm", align_bytes=64)
+        nc.scalar.activation(out=warm[:], in_=warm_in[:], func=ACT.Relu)
+        nc.sync.dma_start(out=bn_few[0:P:8, :], in_=bn[0, :].partition_broadcast(16))
+        nc.sync.dma_start(out=bn_all[:], in_=bn_few[0:P:8, :].unsqueeze(1).to_broadcast([16, 8, N]))
 
         nc.vector.tensor_copy(
-            out=w_bf[:].rearrange("p (c i) j -> p c j i", i=4),
-            in_=w_raw[:].rearrange("p j (c i) -> p c j i", i=4),
+            out=w_bf[0:U].rearrange("p s (c i) j -> p (s c) j i", i=4),
+            in_=w_raw[0:U].rearrange("p j s (c i) -> p (s c) j i", i=4),
         )
-        x_out = x_bf[:].rearrange("p t g q j -> p g q j t")
-        x_in = x_raw[:].rearrange("p g j (q t) -> p g q j t", t=PACK)
-        nc.vector.tensor_copy(out=x_out[:, 0:2], in_=x_in[:, 0:2])
-        nc.scalar.copy(out=x_out[:, 3], in_=x_in[:, 3])
-        nc.vector.tensor_copy(out=x_out[:, 2], in_=x_in[:, 2])
-        quantize(w_codes[:], w_scales[:], w_bf[:].rearrange("p c j -> p (c j)"))
+        x_out = x_bf[0:U].rearrange("p t g q j -> p g q j t")
+        x_in = [x_raw[m][0:U].rearrange("p g j (q t) -> p g q j t", t=PACK) for m in range(2)]
+        nc.vector.tensor_copy(out=x_out[:, 0], in_=x_in[0][:, 0])
+        nc.scalar.copy(out=x_out[:, 1], in_=x_in[0][:, 1])
+        for s in range(2):
+            quantize(w_codes[0:U, s, :], w_scales[0:U, s, :], w_bf[0:U, s].rearrange("p c j -> p (c j)"))
+        nc.vector.tensor_copy(out=x_out[:, 2], in_=x_in[1][:, 0])
+        nc.vector.tensor_copy(out=x_out[:, 3, 0:XCUT], in_=x_in[1][:, 1, 0:XCUT])
+        nc.scalar.copy(out=x_out[:, 3, XCUT:R], in_=x_in[1][:, 1, XCUT:R])
         nc.scalar.copy(
-            out=ad_bf[:].rearrange("p u e t -> p e t u"),
-            in_=ad_raw[:].rearrange("p t (e u) -> p e t u", u=PACK),
+            out=ad_bf[:].rearrange("p (c i) t -> p c t i", i=4),
+            in_=ad_raw[:].rearrange("p t (c i) -> p c t i", i=4),
         )
-        for t in range(PACK):
-            quantize(x_codes[:, t, :], x_scales[:, t, :], x_bf[:, t].rearrange("p g q j -> p (g q j)"))
-            for r in range(4):
+
+        def z_bank(r):
+            return (bank_a if r < 2 else bank_b)[2 * (r % 2)]
+
+        def first_product(t, chunks):
+            for s, b in [divmod(r, 2) for r in chunks]:
                 nc.tensor.matmul_mx(
-                    out=bank_a[r][:, t, :],
-                    lhsT=x_codes[rows(r), t, :].bitcast(FP8X4),
-                    lhsT_scale=x_scales[rows(r), t, :],
-                    rhs=w_codes[rows(r), :].bitcast(FP8X4),
-                    rhs_scale=w_scales[rows(r), :],
+                    out=z_bank(2 * s + b)[:, t, :],
+                    lhsT=x_codes[rows(2 * b), t, :].bitcast(FP8X4),
+                    lhsT_scale=x_scales[rows(2 * b), t, :],
+                    rhs=w_codes[rows(2 * b), s, :].bitcast(FP8X4),
+                    rhs_scale=w_scales[rows(2 * b), s, :],
                     start=True,
                     stop=True,
                 )
-        quantize(ad_codes[:], ad_scales[:], ad_bf[:].rearrange("p u e t -> p (u e t)"))
-        nc.vector.transpose(bn_cols[:], bn_rows[:])
 
         for t in range(PACK):
-            nc.scalar.activation(
-                out=h_bf[:, :, 3, :, t],
-                in_=bank_a[3][:, t, :].rearrange("p (k c) -> p k c", k=4),
-                func=ACT.Copy,
-                scale=ni_sb[:, t : t + 1],
-            )
-        for a in range(3):
+            quantize(x_codes[0:U, t, :], x_scales[0:U, t, :], x_bf[0:U, t].rearrange("p g q j -> p (g q j)"))
+            first_product(t, (2, 1))
+        for t in range(PACK):
+            first_product(t, (0, 3))
+        quantize(ad_codes[:], ad_scales[:], ad_bf[:].rearrange("p j t -> p (j t)"))
+
+        def y_bank(g, h):
+            return bank_a[g][:, 0:2, :] if h == 0 else bank_b[g][:, 0:2, :]
+
+        def scale_h(r):
             nc.vector.tensor_tensor(
-                out=h_bf[:, :, a],
-                in0=bank_a[a][:].rearrange("p t (k c) -> p k c t", k=4),
-                in1=ni_sb[:].unsqueeze(1).unsqueeze(1).to_broadcast([P, 4, R, PACK]),
+                out=h_bf[:, r],
+                in0=z_bank(r)[:].rearrange("p t c -> p c t"),
+                in1=ni_sb[:].unsqueeze(1).to_broadcast([P, C, PACK]),
                 op=ALU.mult,
             )
 
-        def y_bank(g, k):
-            return bank_b[g][:, k, :] if k < 2 else bank_a[g][:, k, :]
+        def quantize_h(r):
+            quantize(h_codes[:, r, :], h_scales[:, r, :], h_bf[:, r].rearrange("p c t -> p (c t)"))
 
-        for half in range(2):
-            ks = slice(2 * half, 2 * half + 2)
-            quantize(
-                h_codes[:, ks].rearrange("p k c -> p (k c)"),
-                h_scales[:, ks].rearrange("p k c -> p (k c)"),
-                h_bf[:, ks].rearrange("p k a c t -> p (k a c t)"),
-            )
-            for k in (2 * half, 2 * half + 1):
-                for g in range(G):
-                    nc.tensor.matmul_mx(
-                        out=y_bank(g, k),
-                        lhsT=h_codes[rows(g), k, :].bitcast(FP8X4),
-                        lhsT_scale=h_scales[rows(g), k, :],
-                        rhs=ad_codes[rows(g), :].bitcast(FP8X4),
-                        rhs_scale=ad_scales[rows(g), :],
-                        start=True,
-                        stop=True,
-                    )
-
-        def relu(g, k, on_vector):
-            src = y_bank(g, k).rearrange("p (u e) -> p u e", u=PACK)
-            bias = bn_cols[:, R * k : R * k + 1]
-            if on_vector:
-                nc.vector.tensor_scalar(
-                    out=y_t[g][:, :, k, :], in0=src, scalar1=bias, scalar2=0.0, op0=ALU.add, op1=ALU.max
+        def second_product(r):
+            for g in (0, 2, 1, 3):
+                nc.tensor.matmul_mx(
+                    out=y_bank(g, r // 2)[:, r % 2, :],
+                    lhsT=ad_codes[rows(g), :].bitcast(FP8X4),
+                    lhsT_scale=ad_scales[rows(g), :],
+                    rhs=h_codes[rows(g), r, :].bitcast(FP8X4),
+                    rhs_scale=h_scales[rows(g), r, :],
+                    start=True,
+                    stop=True,
                 )
-            else:
-                nc.scalar.activation(out=y_t[g][:, :, k, :], in_=src, func=ACT.Relu, bias=bias)
 
-        out_rows = out_0.rearrange("(g e u) (a n) -> g a e u n", g=G, u=PACK, a=4)
-
-        def turn_and_store(g):
-            nc.vector.transpose(
-                y_f[g][:].rearrange("p u n -> p (u n)"), y_t[g][:].rearrange("p u k e -> p (u k e)")
+        for t in range(PACK):
+            nc.scalar.activation(
+                out=h_bf[:, 2, :, t], in_=z_bank(2)[:, t, :], func=ACT.Copy, scale=ni_sb[:, t : t + 1]
             )
-            for a in (0, 2, 1, 3):
-                nc.sync.dma_start(out=out_rows[g, a], in_=y_f[g][rows(a)])
+        scale_h(1)
+        scale_h(0)
+        quantize_h(1)
+        quantize_h(0)
+        second_product(1)
+        second_product(0)
+        scale_h(3)
+        quantize_h(2)
+        quantize_h(3)
+        second_product(2)
+        second_product(3)
 
-        def round_y(g, on_vector):
-            dst = y_bf[g][:].rearrange("p (c i) u -> p c u i", i=4)
-            src = y_f[g][:].rearrange("p u (c i) -> p c u i", i=4)
-            if on_vector:
-                nc.vector.tensor_copy(out=dst, in_=src)
-            else:
-                nc.scalar.copy(out=dst, in_=src)
+        for h in range(2):
+            cols = slice(H * h, H * h + H)
+            for g in (0, 2, 1, 3):
+                nc.vector.tensor_tensor(
+                    out=sums[h][g][:],
+                    in0=y_bank(g, h).rearrange("p r c -> p (r c)"),
+                    in1=bn_all[:, cols],
+                    op=ALU.add,
+                )
+                queue[g].dma_start(out=grouped[h][rows(g)], in_=sums[h][g][:])
+                nc.scalar.activation(out=y_f[g][:, cols], in_=sums[h][g][:], func=ACT.Relu)
+        for g in (0, 2, 1, 3):
+            nc.sync.dma_start(out=out_0[J * g : J * g + J, :], in_=y_f[g][:])
 
-        def quantize_y(g):
-            quantize(y_codes[:, g, :], y_scales[:, g, :], y_bf[g][:].rearrange("p n u -> p (n u)"))
-
+        words = out_1.rearrange("s p n u -> (s p) (n u)").bitcast(I32)
+        scale_rows = out_2.rearrange("s f n -> (s f) n").bitcast(I32)
+        for h in range(2):
+            cols = slice(H * h, H * h + H)
+            dst = y_bf[h][:].rearrange("p (c i) u -> p c u i", i=4)
+            src = grouped[h][:].rearrange("p u (c i) -> p c u i", i=4)
+            cut = SPLIT // 4
+            nc.vector.tensor_scalar(out=dst[:, :cut], in0=src[:, :cut], scalar1=0.0, scalar2=None, op0=ALU.max)
+            nc.scalar.activation(out=dst[:, cut:], in_=src[:, cut:], func=ACT.Relu)
+            quantize(y_codes[:, cols], y_scales[:, cols], y_bf[h][:].rearrange("p n u -> p (n u)"))
+            nc.sync.dma_start(out=words[:, cols], in_=y_codes[:, cols].bitcast(I32))
         for g in range(G):
-            for k in range(4):
-                relu(g, k, g == 0 and k >= 2)
-        turn_and_store(0)
-        turn_and_store(1)
-        round_y(0, True)
-        turn_and_store(2)
-        round_y(1, False)
-        quantize_y(0)
-        turn_and_store(3)
-        round_y(2, False)
-        quantize_y(1)
-        round_y(3, True)
-        quantize_y(2)
-        quantize_y(3)
-
-        words = out_1.rearrange("s p n u -> (s p) (n u)").bitcast(I32).rearrange("(g e) (a n) -> a e g n", g=G, a=4)
-        scale_rows = out_2.rearrange("s f n -> (s f) n").bitcast(I32).rearrange("(g f) (a n) -> a f g n", g=G, a=4)
-        for a in (0, 2, 1, 3):
-            queue[a].dma_start(out=words[a], in_=y_codes[rows(a)].bitcast(I32))
-        for a in (0, 2, 1, 3):
-            queue[a].dma_start(out=scale_rows[a], in_=y_scales[R * a : R * a + 4].bitcast(I32))
+            queue[3 - g].dma_start(out=scale_rows[4 * g : 4 * g + 4, :], in_=y_scales[R * g : R * g + 4, :].bitcast(I32))

@@ -62,9 +62,10 @@ def tile_rows_pl_gnn_gcn_kernel(tc, x, w, ni, ad, bn, out_0, out_1, out_2):
         y_codes = sb.tile([P, N], U32, name="y_codes", align_bytes=64)
         y_scales = sb.tile([P, N], U8, name="y_scales", align_bytes=64)
 
-        sums = [[sb.tile([P, H], F32, name="sums%d_%d" % (h, g), align_bytes=64) for g in range(G)] for h in range(2)]
+        sums = [sb.tile([P, N], F32, name="sums%d" % g, align_bytes=64) for g in range(G)]
+        rounded = [[sb.tile([P, H], BF16, name="rounded%d_%d" % (h, g), align_bytes=64) for g in range(G)] for h in range(2)]
         y_f = [sb.tile([P, N], F32, name="y_f%d" % g, align_bytes=64) for g in range(G)]
-        grouped = [sb.tile([P, PACK, H], F32, name="grouped%d" % h, align_bytes=64) for h in range(2)]
+        grouped = [sb.tile([P, PACK, H], BF16, name="grouped%d" % h, align_bytes=64) for h in range(2)]
         y_bf = [sb.tile([P, H, PACK], BF16, name="y_bf%d" % h, align_bytes=64) for h in range(2)]
 
         bank_a = [ps.tile([P, 4, C], F32, name="bank_a%d" % r) for r in range(4)]
@@ -98,15 +99,15 @@ def tile_rows_pl_gnn_gcn_kernel(tc, x, w, ni, ad, bn, out_0, out_1, out_2):
             out=w_bf[0:U].rearrange("p s (c i) j -> p (s c) j i", i=4),
             in_=w_raw[0:U].rearrange("p j s (c i) -> p (s c) j i", i=4),
         )
-        x_out = x_bf[0:U].rearrange("p t g q j -> p g q j t")
-        x_in = [x_raw[m][0:U].rearrange("p g j (q t) -> p g q j t", t=PACK) for m in range(2)]
+        x_out = x_bf[0:U].rearrange("p (a b) g q j -> p g a q j b", b=2)
+        x_in = [x_raw[m][0:U].rearrange("p g j (q a b) -> p g a q j b", a=2, b=2) for m in range(2)]
         nc.vector.tensor_copy(out=x_out[:, 0], in_=x_in[0][:, 0])
         nc.scalar.copy(out=x_out[:, 1], in_=x_in[0][:, 1])
         for s in range(2):
             quantize(w_codes[0:U, s, :], w_scales[0:U, s, :], w_bf[0:U, s].rearrange("p c j -> p (c j)"))
         nc.vector.tensor_copy(out=x_out[:, 2], in_=x_in[1][:, 0])
-        nc.vector.tensor_copy(out=x_out[:, 3, 0:XCUT], in_=x_in[1][:, 1, 0:XCUT])
-        nc.scalar.copy(out=x_out[:, 3, XCUT:R], in_=x_in[1][:, 1, XCUT:R])
+        nc.vector.tensor_copy(out=x_out[:, 3, :, 0:XCUT], in_=x_in[1][:, 1, :, 0:XCUT])
+        nc.scalar.copy(out=x_out[:, 3, :, XCUT:R], in_=x_in[1][:, 1, :, XCUT:R])
         nc.scalar.copy(
             out=ad_bf[:].rearrange("p (c i) t -> p c t i", i=4),
             in_=ad_raw[:].rearrange("p t (c i) -> p c t i", i=4),
@@ -139,9 +140,9 @@ def tile_rows_pl_gnn_gcn_kernel(tc, x, w, ni, ad, bn, out_0, out_1, out_2):
 
         def scale_h(r):
             nc.vector.tensor_tensor(
-                out=h_bf[:, r],
-                in0=z_bank(r)[:].rearrange("p t c -> p c t"),
-                in1=ni_sb[:].unsqueeze(1).to_broadcast([P, C, PACK]),
+                out=h_bf[:, r].rearrange("p (c i) t -> p c t i", i=2),
+                in0=z_bank(r)[:].rearrange("p t (c i) -> p c t i", i=2),
+                in1=ni_sb[:].unsqueeze(1).unsqueeze(3).to_broadcast([P, C // 2, PACK, 2]),
                 op=ALU.mult,
             )
 
@@ -180,14 +181,15 @@ def tile_rows_pl_gnn_gcn_kernel(tc, x, w, ni, ad, bn, out_0, out_1, out_2):
             cols = slice(H * h, H * h + H)
             for g in (0, 2, 1, 3):
                 nc.vector.tensor_tensor(
-                    out=sums[h][g][:],
+                    out=sums[g][:, cols],
                     in0=y_bank(g, h).rearrange("p r c -> p (r c)"),
                     in1=bn_all[:, cols],
                     op=ALU.add,
                 )
-                queue[g].dma_start(out=grouped[h][rows(g)], in_=sums[h][g][:])
-                nc.scalar.activation(out=y_f[g][:, cols], in_=sums[h][g][:], func=ACT.Relu)
+                nc.scalar.activation(out=rounded[h][g][:], in_=sums[g][:, cols], func=ACT.Relu)
+                nc.sync.dma_start(out=grouped[h][rows(g)], in_=rounded[h][g][:])
         for g in (0, 2, 1, 3):
+            nc.vector.tensor_scalar(out=y_f[g][:], in0=sums[g][:], scalar1=0.0, scalar2=None, op0=ALU.max)
             nc.sync.dma_start(out=out_0[J * g : J * g + J, :], in_=y_f[g][:])
 
         words = out_1.rearrange("s p n u -> (s p) (n u)").bitcast(I32)
@@ -197,9 +199,9 @@ def tile_rows_pl_gnn_gcn_kernel(tc, x, w, ni, ad, bn, out_0, out_1, out_2):
             dst = y_bf[h][:].rearrange("p (c i) u -> p c u i", i=4)
             src = grouped[h][:].rearrange("p u (c i) -> p c u i", i=4)
             cut = SPLIT // 4
-            nc.vector.tensor_scalar(out=dst[:, :cut], in0=src[:, :cut], scalar1=0.0, scalar2=None, op0=ALU.max)
-            nc.scalar.activation(out=dst[:, cut:], in_=src[:, cut:], func=ACT.Relu)
+            nc.vector.tensor_copy(out=dst[:, :cut], in_=src[:, :cut])
+            nc.scalar.copy(out=dst[:, cut:], in_=src[:, cut:])
             quantize(y_codes[:, cols], y_scales[:, cols], y_bf[h][:].rearrange("p n u -> p (n u)"))
-            nc.sync.dma_start(out=words[:, cols], in_=y_codes[:, cols].bitcast(I32))
+            nc.scalar.dma_start(out=words[:, cols], in_=y_codes[:, cols].bitcast(I32))
         for g in range(G):
-            queue[3 - g].dma_start(out=scale_rows[4 * g : 4 * g + 4, :], in_=y_scales[R * g : R * g + 4, :].bitcast(I32))
+            queue[g].dma_start(out=scale_rows[4 * g : 4 * g + 4, :], in_=y_scales[R * g : R * g + 4, :].bitcast(I32))

@@ -21,7 +21,7 @@ C = 128
 H = 256
 SPLIT = 160
 U = 96
-XCUT = 8
+XCUT = 16
 
 
 def tile_rows_pl_gnn_gcn_kernel(tc, x, w, ni, ad, bn, out_0, out_1, out_2):
@@ -85,14 +85,14 @@ def tile_rows_pl_gnn_gcn_kernel(tc, x, w, ni, ad, bn, out_0, out_1, out_2):
         for m in range(2):
             for b in range(2):
                 queue[2 * b].dma_start(out=x_raw[m][rows(2 * b)].rearrange("p g j i -> p g (j i)"), in_=x_rows[m])
+        nc.sync.dma_start(out=ni_sb[:], in_=ni.rearrange("g (p t) o -> (g p) (t o)", t=PACK))
+        nc.scalar.dma_start(out=bn_few[0:P:8, :], in_=bn[0, :].partition_broadcast(16))
         nc.sync.dma_start(
             out=ad_raw[:].rearrange("p t j -> p (t j)"),
             in_=ad.rearrange("g (p t) j -> (g p) (t j)", t=PACK),
         )
-        nc.scalar.dma_start(out=ni_sb[:], in_=ni.rearrange("g (p t) o -> (g p) (t o)", t=PACK))
         warm = sb.tile([P, 8], F32, name="warm", align_bytes=64)
         nc.scalar.activation(out=warm[:], in_=warm_in[:], func=ACT.Relu)
-        nc.sync.dma_start(out=bn_few[0:P:8, :], in_=bn[0, :].partition_broadcast(16))
         nc.sync.dma_start(out=bn_all[:], in_=bn_few[0:P:8, :].unsqueeze(1).to_broadcast([16, 8, N]))
 
         nc.vector.tensor_copy(
@@ -105,9 +105,10 @@ def tile_rows_pl_gnn_gcn_kernel(tc, x, w, ni, ad, bn, out_0, out_1, out_2):
         nc.scalar.copy(out=x_out[:, 1], in_=x_in[0][:, 1])
         for s in range(2):
             quantize(w_codes[0:U, s, :], w_scales[0:U, s, :], w_bf[0:U, s].rearrange("p c j -> p (c j)"))
-        nc.vector.tensor_copy(out=x_out[:, 2], in_=x_in[1][:, 0])
-        nc.vector.tensor_copy(out=x_out[:, 3, :, 0:XCUT], in_=x_in[1][:, 1, :, 0:XCUT])
-        nc.scalar.copy(out=x_out[:, 3, :, XCUT:R], in_=x_in[1][:, 1, :, XCUT:R])
+        nc.vector.tensor_copy(out=x_out[:, 2:4, 0], in_=x_in[1][:, :, 0])
+        nc.vector.tensor_copy(out=x_out[:, 2, 1, 0:XCUT], in_=x_in[1][:, 0, 1, 0:XCUT])
+        nc.scalar.copy(out=x_out[:, 2, 1, XCUT:R], in_=x_in[1][:, 0, 1, XCUT:R])
+        nc.scalar.copy(out=x_out[:, 3, 1], in_=x_in[1][:, 1, 1])
         nc.scalar.copy(
             out=ad_bf[:].rearrange("p (c i) t -> p c t i", i=4),
             in_=ad_raw[:].rearrange("p t (c i) -> p c t i", i=4),
@@ -149,8 +150,8 @@ def tile_rows_pl_gnn_gcn_kernel(tc, x, w, ni, ad, bn, out_0, out_1, out_2):
         def quantize_h(r):
             quantize(h_codes[:, r, :], h_scales[:, r, :], h_bf[:, r].rearrange("p c t -> p (c t)"))
 
-        def second_product(r):
-            for g in (0, 2, 1, 3):
+        def second_product(*chunks):
+            for g, r in [(g, r) for g in (0, 2, 1, 3) for r in chunks]:
                 nc.tensor.matmul_mx(
                     out=y_bank(g, r // 2)[:, r % 2, :],
                     lhsT=ad_codes[rows(g), :].bitcast(FP8X4),
@@ -169,28 +170,39 @@ def tile_rows_pl_gnn_gcn_kernel(tc, x, w, ni, ad, bn, out_0, out_1, out_2):
         scale_h(0)
         quantize_h(1)
         quantize_h(0)
-        second_product(1)
-        second_product(0)
+        second_product(1, 0)
         scale_h(3)
         quantize_h(2)
-        quantize_h(3)
         second_product(2)
-        second_product(3)
 
+        def add_bias(dst, g, h):
+            nc.vector.tensor_tensor(
+                out=dst,
+                in0=y_bank(g, h).rearrange("p r c -> p (r c)"),
+                in1=bn_all[:, H * h : H * h + H],
+                op=ALU.add,
+            )
+
+        order = (0, 2, 1, 3)
         for h in range(2):
             cols = slice(H * h, H * h + H)
-            for g in (0, 2, 1, 3):
-                nc.vector.tensor_tensor(
-                    out=sums[g][:, cols],
-                    in0=y_bank(g, h).rearrange("p r c -> p (r c)"),
-                    in1=bn_all[:, cols],
-                    op=ALU.add,
-                )
-                nc.scalar.activation(out=rounded[h][g][:], in_=sums[g][:, cols], func=ACT.Relu)
+            for g in order:
+                if h == 1 and g in order[2:]:
+                    add_bias(rounded[h][g][:], g, h)
+                else:
+                    add_bias(sums[g][:, cols], g, h)
+                    nc.scalar.copy(out=rounded[h][g][:], in_=sums[g][:, cols])
                 nc.sync.dma_start(out=grouped[h][rows(g)], in_=rounded[h][g][:])
-        for g in (0, 2, 1, 3):
-            nc.vector.tensor_scalar(out=y_f[g][:], in0=sums[g][:], scalar1=0.0, scalar2=None, op0=ALU.max)
+                if h == 0 and g == order[0]:
+                    quantize_h(3)
+                    second_product(3)
+        for g in order[2:]:
+            add_bias(sums[g][:, H:N], g, 1)
+        for g, other in zip(order[:2], order[2:]):
+            nc.scalar.activation(out=y_f[g][:], in_=sums[g][:], func=ACT.Relu)
             nc.sync.dma_start(out=out_0[J * g : J * g + J, :], in_=y_f[g][:])
+            nc.vector.tensor_scalar(out=y_f[other][:], in0=sums[other][:], scalar1=0.0, scalar2=None, op0=ALU.max)
+            nc.sync.dma_start(out=out_0[J * other : J * other + J, :], in_=y_f[other][:])
 
         words = out_1.rearrange("s p n u -> (s p) (n u)").bitcast(I32)
         scale_rows = out_2.rearrange("s f n -> (s f) n").bitcast(I32)
@@ -199,8 +211,10 @@ def tile_rows_pl_gnn_gcn_kernel(tc, x, w, ni, ad, bn, out_0, out_1, out_2):
             dst = y_bf[h][:].rearrange("p (c i) u -> p c u i", i=4)
             src = grouped[h][:].rearrange("p u (c i) -> p c u i", i=4)
             cut = SPLIT // 4
-            nc.vector.tensor_copy(out=dst[:, :cut], in_=src[:, :cut])
-            nc.scalar.copy(out=dst[:, cut:], in_=src[:, cut:])
+            nc.vector.tensor_scalar(out=dst[:, :cut], in0=src[:, :cut], scalar1=0.0, scalar2=None, op0=ALU.max)
+            nc.scalar.activation(out=dst[:, cut:], in_=src[:, cut:], func=ACT.Relu)
+        for h in range(2):
+            cols = slice(H * h, H * h + H)
             quantize(y_codes[:, cols], y_scales[:, cols], y_bf[h][:].rearrange("p n u -> p (n u)"))
             nc.scalar.dma_start(out=words[:, cols], in_=y_codes[:, cols].bitcast(I32))
         for g in range(G):

@@ -18,10 +18,14 @@ P = 128
 R = 32
 PACK = 4
 C = 128
-H = 256
-SPLIT = 160
-U = 96
-XCUT = 16
+CHUNKS = N // C
+H = N // 2
+SPAN = 3 * R
+BN_COPIES = 16
+RUN = 4
+VECTOR_COLUMNS = 160
+SCALAR_FILL = 8
+GRAPH_ORDER = (0, 2, 1, 3)
 
 
 def tile_rows_pl_gnn_gcn_kernel(tc, x, w, ni, ad, bn, out_0, out_1, out_2):
@@ -29,6 +33,9 @@ def tile_rows_pl_gnn_gcn_kernel(tc, x, w, ni, ad, bn, out_0, out_1, out_2):
 
     def rows(r):
         return slice(R * r, R * r + R)
+
+    def half_columns(h):
+        return slice(H * h, H * h + H)
 
     def quantize(codes, scales, src):
         nc.vector.quantize_mx(out=codes.bitcast(FP8X4), scales=scales, in_=src)
@@ -38,184 +45,211 @@ def tile_rows_pl_gnn_gcn_kernel(tc, x, w, ni, ad, bn, out_0, out_1, out_2):
         ps = ctx.enter_context(tc.psum_pool(name="ps", bufs=1))
         ctx.enter_context(tc.manual_schedule())
 
-        x_raw = [sb.tile([P, 2, PACK, I], F32, name="x_raw%d" % m, align_bytes=64) for m in range(2)]
-        w_raw = sb.tile([P, PACK, 2, C], F32, name="w_raw", align_bytes=64)
-        ad_raw = sb.tile([P, PACK, J], F32, name="ad_raw", align_bytes=64)
-        ni_sb = sb.tile([P, PACK], F32, name="ni_sb", align_bytes=64)
-        bn_few = sb.tile([P, N], F32, name="bn_few", align_bytes=64)
-        bn_all = sb.tile([P, N], F32, name="bn_all", align_bytes=64)
-        warm_in = sb.tile([P, 8], F32, name="warm_in", align_bytes=64)
+        def sbuf(name, shape, dtype):
+            return sb.tile(shape, dtype, name=name, align_bytes=64)
 
-        x_bf = sb.tile([P, PACK, G, R, PACK], BF16, name="x_bf", align_bytes=64)
-        w_bf = sb.tile([P, 2, C, PACK], BF16, name="w_bf", align_bytes=64)
-        ad_bf = sb.tile([P, J, PACK], BF16, name="ad_bf", align_bytes=64)
-        h_bf = sb.tile([P, 4, C, PACK], BF16, name="h_bf", align_bytes=64)
+        x_raw = [sbuf("x_raw%d" % m, [P, 2, PACK, I], F32) for m in range(2)]
+        w_raw = sbuf("w_raw", [P, PACK, 2, C], F32)
+        ad_raw = sbuf("ad_raw", [P, PACK, J], F32)
+        ni_sb = sbuf("ni_sb", [P, PACK], F32)
+        bn_few = sbuf("bn_few", [P, N], F32)
+        bn_all = sbuf("bn_all", [P, N], F32)
+        zeros = sbuf("zeros", [P, SCALAR_FILL], F32)
 
-        x_codes = sb.tile([P, PACK, C], U32, name="x_codes", align_bytes=64)
-        x_scales = sb.tile([P, PACK, C], U8, name="x_scales", align_bytes=64)
-        w_codes = sb.tile([P, 2, C], U32, name="w_codes", align_bytes=64)
-        w_scales = sb.tile([P, 2, C], U8, name="w_scales", align_bytes=64)
-        ad_codes = sb.tile([P, J], U32, name="ad_codes", align_bytes=64)
-        ad_scales = sb.tile([P, J], U8, name="ad_scales", align_bytes=64)
-        h_codes = sb.tile([P, 4, C], U32, name="h_codes", align_bytes=64)
-        h_scales = sb.tile([P, 4, C], U8, name="h_scales", align_bytes=64)
-        y_codes = sb.tile([P, N], U32, name="y_codes", align_bytes=64)
-        y_scales = sb.tile([P, N], U8, name="y_scales", align_bytes=64)
+        x_bf = sbuf("x_bf", [P, PACK, G, R, PACK], BF16)
+        w_bf = sbuf("w_bf", [P, 2, C, PACK], BF16)
+        ad_bf = sbuf("ad_bf", [P, J, PACK], BF16)
+        h_bf = sbuf("h_bf", [P, CHUNKS, C, PACK], BF16)
 
-        sums = [sb.tile([P, N], F32, name="sums%d" % g, align_bytes=64) for g in range(G)]
-        rounded = [[sb.tile([P, H], BF16, name="rounded%d_%d" % (h, g), align_bytes=64) for g in range(G)] for h in range(2)]
-        y_f = [sb.tile([P, N], F32, name="y_f%d" % g, align_bytes=64) for g in range(G)]
-        grouped = [sb.tile([P, PACK, H], BF16, name="grouped%d" % h, align_bytes=64) for h in range(2)]
-        y_bf = [sb.tile([P, H, PACK], BF16, name="y_bf%d" % h, align_bytes=64) for h in range(2)]
+        x_codes = sbuf("x_codes", [P, PACK, G * R], U32)
+        x_scales = sbuf("x_scales", [P, PACK, G * R], U8)
+        w_codes = sbuf("w_codes", [P, 2, C], U32)
+        w_scales = sbuf("w_scales", [P, 2, C], U8)
+        ad_codes = sbuf("ad_codes", [P, J], U32)
+        ad_scales = sbuf("ad_scales", [P, J], U8)
+        h_codes = sbuf("h_codes", [P, CHUNKS, C], U32)
+        h_scales = sbuf("h_scales", [P, CHUNKS, C], U8)
+        y_codes = sbuf("y_codes", [P, N], U32)
+        y_scales = sbuf("y_scales", [P, N], U8)
 
-        bank_a = [ps.tile([P, 4, C], F32, name="bank_a%d" % r) for r in range(4)]
-        bank_b = [ps.tile([P, 4, C], F32, name="bank_b%d" % r) for r in range(4)]
+        sums = [sbuf("sums%d" % g, [P, N], F32) for g in range(G)]
+        rounded = [[sbuf("rounded%d_%d" % (h, g), [P, H], BF16) for g in range(G)] for h in range(2)]
+        y_out = [sbuf("y_out%d" % g, [P, N], F32) for g in range(G)]
+        grouped = [sbuf("grouped%d" % h, [P, PACK, H], BF16) for h in range(2)]
+        y_bf = [sbuf("y_bf%d" % h, [P, H, PACK], BF16) for h in range(2)]
 
-        nc.gpsimd.memset(warm_in[:], 0.0)
+        bank_a = [ps.tile([P, PACK, C], F32, name="bank_a%d" % r) for r in range(G)]
+        bank_b = [ps.tile([P, PACK, C], F32, name="bank_b%d" % r) for r in range(G)]
 
+        x_fill = x_raw[1][rows(1)].rearrange("p g j i -> p (g j i)")
+        fill_cut = 2 * PACK * I - SCALAR_FILL
+        nc.gpsimd.memset(zeros[rows(1)], 0.0)
         nc.vector.memset(w_raw[rows(1)].bitcast(I32), 0)
         nc.vector.memset(x_raw[0][rows(1)].bitcast(I32), 0)
-        nc.gpsimd.memset(x_raw[1][rows(1)].bitcast(I32), 0)
+        nc.gpsimd.memset(x_fill[:, :fill_cut].bitcast(I32), 0)
 
-        queue = [nc.sync, nc.sync, nc.scalar, nc.scalar]
+        tile_queue = [nc.sync, nc.scalar]
         w_rows = w.rearrange("(p j) (s b n) -> b p (j s) n", j=PACK, s=2, b=2)
         x_rows = x.rearrange("(m g) (p j) i -> m p g (j i)", m=2, j=PACK)
         for b in range(2):
-            queue[2 * b].dma_start(out=w_raw[rows(2 * b)].rearrange("p j s n -> p (j s) n"), in_=w_rows[b])
+            tile_queue[b].dma_start(out=w_raw[rows(2 * b)].rearrange("p j s n -> p (j s) n"), in_=w_rows[b])
         for m in range(2):
             for b in range(2):
-                queue[2 * b].dma_start(out=x_raw[m][rows(2 * b)].rearrange("p g j i -> p g (j i)"), in_=x_rows[m])
+                tile_queue[b].dma_start(out=x_raw[m][rows(2 * b)].rearrange("p g j i -> p g (j i)"), in_=x_rows[m])
         nc.sync.dma_start(out=ni_sb[:], in_=ni.rearrange("g (p t) o -> (g p) (t o)", t=PACK))
-        nc.scalar.dma_start(out=bn_few[0:P:8, :], in_=bn[0, :].partition_broadcast(16))
+        bn_step = P // BN_COPIES
+        nc.scalar.dma_start(out=bn_few[0:P:bn_step, :], in_=bn[0, :].partition_broadcast(BN_COPIES))
         nc.sync.dma_start(
             out=ad_raw[:].rearrange("p t j -> p (t j)"),
             in_=ad.rearrange("g (p t) j -> (g p) (t j)", t=PACK),
         )
-        warm = sb.tile([P, 8], F32, name="warm", align_bytes=64)
-        nc.scalar.activation(out=warm[:], in_=warm_in[:], func=ACT.Relu)
-        nc.sync.dma_start(out=bn_all[:], in_=bn_few[0:P:8, :].unsqueeze(1).to_broadcast([16, 8, N]))
+        nc.scalar.activation(out=x_fill[:, fill_cut:], in_=zeros[rows(1)], func=ACT.Relu)
+        nc.sync.dma_start(
+            out=bn_all[:], in_=bn_few[0:P:bn_step, :].unsqueeze(1).to_broadcast([BN_COPIES, bn_step, N])
+        )
 
         nc.vector.tensor_copy(
-            out=w_bf[0:U].rearrange("p s (c i) j -> p (s c) j i", i=4),
-            in_=w_raw[0:U].rearrange("p j s (c i) -> p (s c) j i", i=4),
+            out=w_bf[0:SPAN].rearrange("p s (c i) j -> p (s c) j i", i=RUN),
+            in_=w_raw[0:SPAN].rearrange("p j s (c i) -> p (s c) j i", i=RUN),
         )
-        x_out = x_bf[0:U].rearrange("p (a b) g q j -> p g a q j b", b=2)
-        x_in = [x_raw[m][0:U].rearrange("p g j (q a b) -> p g a q j b", a=2, b=2) for m in range(2)]
-        nc.vector.tensor_copy(out=x_out[:, 0], in_=x_in[0][:, 0])
-        nc.scalar.copy(out=x_out[:, 1], in_=x_in[0][:, 1])
-        for s in range(2):
-            quantize(w_codes[0:U, s, :], w_scales[0:U, s, :], w_bf[0:U, s].rearrange("p c j -> p (c j)"))
-        nc.vector.tensor_copy(out=x_out[:, 2:4, 0], in_=x_in[1][:, :, 0])
-        nc.vector.tensor_copy(out=x_out[:, 2, 1, 0:XCUT], in_=x_in[1][:, 0, 1, 0:XCUT])
-        nc.scalar.copy(out=x_out[:, 2, 1, XCUT:R], in_=x_in[1][:, 0, 1, XCUT:R])
-        nc.scalar.copy(out=x_out[:, 3, 1], in_=x_in[1][:, 1, 1])
+        x_dst = x_bf[0:SPAN].rearrange("p (a b) g q j -> p g a q j b", b=2)
+        x_src = [x_raw[m][0:SPAN].rearrange("p g j (q a b) -> p g a q j b", a=2, b=2) for m in range(2)]
+
+        def quantize_w(s):
+            quantize(w_codes[0:SPAN, s, :], w_scales[0:SPAN, s, :], w_bf[0:SPAN, s].rearrange("p c j -> p (c j)"))
+
+        nc.vector.tensor_copy(out=x_dst[:, 0], in_=x_src[0][:, 0])
+        nc.scalar.copy(out=x_dst[:, 1], in_=x_src[0][:, 1])
+        quantize_w(0)
+        nc.vector.tensor_copy(out=x_dst[:, 2:4, 0], in_=x_src[1][:, :, 0])
+        nc.scalar.copy(out=x_dst[:, 2:4, 1], in_=x_src[1][:, :, 1])
+        quantize_w(1)
         nc.scalar.copy(
-            out=ad_bf[:].rearrange("p (c i) t -> p c t i", i=4),
-            in_=ad_raw[:].rearrange("p t (c i) -> p c t i", i=4),
+            out=ad_bf[:].rearrange("p (c i) t -> p c t i", i=RUN),
+            in_=ad_raw[:].rearrange("p t (c i) -> p c t i", i=RUN),
         )
 
-        def z_bank(r):
-            return (bank_a if r < 2 else bank_b)[2 * (r % 2)]
+        def z_bank(chunk):
+            s, b = divmod(chunk, 2)
+            return (bank_a, bank_b)[s][2 * b]
 
-        def first_product(t, chunks):
-            for s, b in [divmod(r, 2) for r in chunks]:
-                nc.tensor.matmul_mx(
-                    out=z_bank(2 * s + b)[:, t, :],
-                    lhsT=x_codes[rows(2 * b), t, :].bitcast(FP8X4),
-                    lhsT_scale=x_scales[rows(2 * b), t, :],
-                    rhs=w_codes[rows(2 * b), s, :].bitcast(FP8X4),
-                    rhs_scale=w_scales[rows(2 * b), s, :],
-                    start=True,
-                    stop=True,
-                )
+        def first_product(t, chunk):
+            s, b = divmod(chunk, 2)
+            nc.tensor.matmul_mx(
+                out=z_bank(chunk)[:, t, :],
+                lhsT=x_codes[rows(2 * b), t, :].bitcast(FP8X4),
+                lhsT_scale=x_scales[rows(2 * b), t, :],
+                rhs=w_codes[rows(2 * b), s, :].bitcast(FP8X4),
+                rhs_scale=w_scales[rows(2 * b), s, :],
+                start=True,
+                stop=True,
+            )
 
         for t in range(PACK):
-            quantize(x_codes[0:U, t, :], x_scales[0:U, t, :], x_bf[0:U, t].rearrange("p g q j -> p (g q j)"))
-            first_product(t, (2, 1))
-        for t in range(PACK):
-            first_product(t, (0, 3))
-        quantize(ad_codes[:], ad_scales[:], ad_bf[:].rearrange("p j t -> p (j t)"))
+            quantize(x_codes[0:SPAN, t, :], x_scales[0:SPAN, t, :], x_bf[0:SPAN, t].rearrange("p g q j -> p (g q j)"))
+            first_product(t, 1)
+            first_product(t, 2)
+        for chunk in (0, 3):
+            for t in range(PACK):
+                first_product(t, chunk)
 
-        def y_bank(g, h):
-            return bank_a[g][:, 0:2, :] if h == 0 else bank_b[g][:, 0:2, :]
-
-        def scale_h(r):
+        def scale_on_vector(chunk):
             nc.vector.tensor_tensor(
-                out=h_bf[:, r].rearrange("p (c i) t -> p c t i", i=2),
-                in0=z_bank(r)[:].rearrange("p t (c i) -> p c t i", i=2),
+                out=h_bf[:, chunk].rearrange("p (c i) t -> p c t i", i=2),
+                in0=z_bank(chunk)[:].rearrange("p t (c i) -> p c t i", i=2),
                 in1=ni_sb[:].unsqueeze(1).unsqueeze(3).to_broadcast([P, C // 2, PACK, 2]),
                 op=ALU.mult,
             )
 
-        def quantize_h(r):
-            quantize(h_codes[:, r, :], h_scales[:, r, :], h_bf[:, r].rearrange("p c t -> p (c t)"))
-
-        def second_product(*chunks):
-            for g, r in [(g, r) for g in (0, 2, 1, 3) for r in chunks]:
-                nc.tensor.matmul_mx(
-                    out=y_bank(g, r // 2)[:, r % 2, :],
-                    lhsT=ad_codes[rows(g), :].bitcast(FP8X4),
-                    lhsT_scale=ad_scales[rows(g), :],
-                    rhs=h_codes[rows(g), r, :].bitcast(FP8X4),
-                    rhs_scale=h_scales[rows(g), r, :],
-                    start=True,
-                    stop=True,
+        def scale_on_scalar(chunk):
+            for t in range(PACK):
+                nc.scalar.activation(
+                    out=h_bf[:, chunk, :, t], in_=z_bank(chunk)[:, t, :], func=ACT.Copy, scale=ni_sb[:, t : t + 1]
                 )
 
-        for t in range(PACK):
-            nc.scalar.activation(
-                out=h_bf[:, 2, :, t], in_=z_bank(2)[:, t, :], func=ACT.Copy, scale=ni_sb[:, t : t + 1]
-            )
-        scale_h(1)
-        scale_h(0)
-        quantize_h(1)
-        quantize_h(0)
-        second_product(1, 0)
-        scale_h(3)
-        quantize_h(2)
-        second_product(2)
+        def quantize_h(chunk):
+            quantize(h_codes[:, chunk, :], h_scales[:, chunk, :], h_bf[:, chunk].rearrange("p c t -> p (c t)"))
+
+        def y_bank(g, h):
+            return (bank_a, bank_b)[h][g][:, 0:2, :]
+
+        def second_product(chunks):
+            for g in GRAPH_ORDER:
+                for chunk in chunks:
+                    nc.tensor.matmul_mx(
+                        out=y_bank(g, chunk // 2)[:, chunk % 2, :],
+                        lhsT=ad_codes[rows(g), :].bitcast(FP8X4),
+                        lhsT_scale=ad_scales[rows(g), :],
+                        rhs=h_codes[rows(g), chunk, :].bitcast(FP8X4),
+                        rhs_scale=h_scales[rows(g), chunk, :],
+                        start=True,
+                        stop=True,
+                    )
 
         def add_bias(dst, g, h):
             nc.vector.tensor_tensor(
                 out=dst,
                 in0=y_bank(g, h).rearrange("p r c -> p (r c)"),
-                in1=bn_all[:, H * h : H * h + H],
+                in1=bn_all[:, half_columns(h)],
                 op=ALU.add,
             )
 
-        order = (0, 2, 1, 3)
+        def regroup(g, h):
+            nc.sync.dma_start(out=grouped[h][rows(g)], in_=rounded[h][g][:])
+
+        def add_round_regroup(g, h):
+            add_bias(sums[g][:, half_columns(h)], g, h)
+            nc.scalar.copy(out=rounded[h][g][:], in_=sums[g][:, half_columns(h)])
+            regroup(g, h)
+
+        scale_on_scalar(2)
+        scale_on_vector(1)
+        scale_on_vector(0)
+        quantize(ad_codes[:], ad_scales[:], ad_bf[:].rearrange("p j t -> p (j t)"))
+        quantize_h(1)
+        quantize_h(0)
+        second_product((1, 0))
+        scale_on_vector(3)
+
+        add_round_regroup(GRAPH_ORDER[0], 0)
+        quantize_h(2)
+        quantize_h(3)
+        second_product((2, 3))
+        for g in GRAPH_ORDER[1:]:
+            add_round_regroup(g, 0)
+
+        early, late = GRAPH_ORDER[:2], GRAPH_ORDER[2:]
+        for g in early:
+            add_round_regroup(g, 1)
+        for g in late:
+            add_bias(rounded[1][g][:], g, 1)
+            regroup(g, 1)
+        for g in late:
+            add_bias(sums[g][:, half_columns(1)], g, 1)
+        for g_early, g_late in zip(early, late):
+            nc.scalar.activation(out=y_out[g_early][:], in_=sums[g_early][:], func=ACT.Relu)
+            nc.sync.dma_start(out=out_0[J * g_early : J * g_early + J, :], in_=y_out[g_early][:])
+            nc.vector.tensor_scalar(
+                out=y_out[g_late][:], in0=sums[g_late][:], scalar1=0.0, scalar2=None, op0=ALU.max
+            )
+            nc.sync.dma_start(out=out_0[J * g_late : J * g_late + J, :], in_=y_out[g_late][:])
+
+        cut = VECTOR_COLUMNS // RUN
         for h in range(2):
-            cols = slice(H * h, H * h + H)
-            for g in order:
-                if h == 1 and g in order[2:]:
-                    add_bias(rounded[h][g][:], g, h)
-                else:
-                    add_bias(sums[g][:, cols], g, h)
-                    nc.scalar.copy(out=rounded[h][g][:], in_=sums[g][:, cols])
-                nc.sync.dma_start(out=grouped[h][rows(g)], in_=rounded[h][g][:])
-                if h == 0 and g == order[0]:
-                    quantize_h(3)
-                    second_product(3)
-        for g in order[2:]:
-            add_bias(sums[g][:, H:N], g, 1)
-        for g, other in zip(order[:2], order[2:]):
-            nc.scalar.activation(out=y_f[g][:], in_=sums[g][:], func=ACT.Relu)
-            nc.sync.dma_start(out=out_0[J * g : J * g + J, :], in_=y_f[g][:])
-            nc.vector.tensor_scalar(out=y_f[other][:], in0=sums[other][:], scalar1=0.0, scalar2=None, op0=ALU.max)
-            nc.sync.dma_start(out=out_0[J * other : J * other + J, :], in_=y_f[other][:])
+            dst = y_bf[h][:].rearrange("p (c i) u -> p c u i", i=RUN)
+            src = grouped[h][:].rearrange("p u (c i) -> p c u i", i=RUN)
+            nc.vector.tensor_scalar(out=dst[:, :cut], in0=src[:, :cut], scalar1=0.0, scalar2=None, op0=ALU.max)
+            nc.scalar.activation(out=dst[:, cut:], in_=src[:, cut:], func=ACT.Relu)
 
         words = out_1.rearrange("s p n u -> (s p) (n u)").bitcast(I32)
         scale_rows = out_2.rearrange("s f n -> (s f) n").bitcast(I32)
         for h in range(2):
-            cols = slice(H * h, H * h + H)
-            dst = y_bf[h][:].rearrange("p (c i) u -> p c u i", i=4)
-            src = grouped[h][:].rearrange("p u (c i) -> p c u i", i=4)
-            cut = SPLIT // 4
-            nc.vector.tensor_scalar(out=dst[:, :cut], in0=src[:, :cut], scalar1=0.0, scalar2=None, op0=ALU.max)
-            nc.scalar.activation(out=dst[:, cut:], in_=src[:, cut:], func=ACT.Relu)
-        for h in range(2):
-            cols = slice(H * h, H * h + H)
+            cols = half_columns(h)
             quantize(y_codes[:, cols], y_scales[:, cols], y_bf[h][:].rearrange("p n u -> p (n u)"))
             nc.scalar.dma_start(out=words[:, cols], in_=y_codes[:, cols].bitcast(I32))
+        blocks = J // 32
         for g in range(G):
-            queue[g].dma_start(out=scale_rows[4 * g : 4 * g + 4, :], in_=y_scales[R * g : R * g + 4, :].bitcast(I32))
+            tile_queue[g // 2].dma_start(
+                out=scale_rows[blocks * g : blocks * g + blocks, :],
+                in_=y_scales[R * g : R * g + blocks, :].bitcast(I32),
+            )

from contextlib import ExitStack

import concourse.mybir as mybir

G, D, I, N, J = 4, 128, 128, 512, 128
FLOPS = 2 * G * I * N * (D + J)

F32 = mybir.dt.float32
BF16 = mybir.dt.bfloat16
I32 = mybir.dt.int32
U32 = mybir.dt.uint32
U8 = mybir.dt.uint8
FP8X4 = mybir.dt.float8_e4m3fn_x4
ACT = mybir.ActivationFunctionType
ALU = mybir.AluOpType

P = 128
R = 32
PACK = 4
C = 128
CHUNKS = N // C
H = N // 2
SPAN = 3 * R
BN_COPIES = 16
RUN = 4
VECTOR_COLUMNS = 160
SCALAR_FILL = 8
GRAPH_ORDER = (0, 2, 1, 3)


def tile_rows_pl_gnn_gcn_kernel(tc, x, w, ni, ad, bn, out_0, out_1, out_2):
    nc = tc.nc

    def rows(r):
        return slice(R * r, R * r + R)

    def half_columns(h):
        return slice(H * h, H * h + H)

    def quantize(codes, scales, src):
        nc.vector.quantize_mx(out=codes.bitcast(FP8X4), scales=scales, in_=src)

    with ExitStack() as ctx:
        sb = ctx.enter_context(tc.tile_pool(name="sb", bufs=1))
        ps = ctx.enter_context(tc.psum_pool(name="ps", bufs=1))
        ctx.enter_context(tc.manual_schedule())

        def sbuf(name, shape, dtype):
            return sb.tile(shape, dtype, name=name, align_bytes=64)

        x_raw = [sbuf("x_raw%d" % m, [P, 2, PACK, I], F32) for m in range(2)]
        w_raw = sbuf("w_raw", [P, PACK, 2, C], F32)
        ad_raw = sbuf("ad_raw", [P, PACK, J], F32)
        ni_sb = sbuf("ni_sb", [P, PACK], F32)
        bn_few = sbuf("bn_few", [P, N], F32)
        bn_all = sbuf("bn_all", [P, N], F32)
        zeros = sbuf("zeros", [P, SCALAR_FILL], F32)

        x_bf = sbuf("x_bf", [P, PACK, G, R, PACK], BF16)
        w_bf = sbuf("w_bf", [P, 2, C, PACK], BF16)
        ad_bf = sbuf("ad_bf", [P, J, PACK], BF16)
        h_bf = sbuf("h_bf", [P, CHUNKS, C, PACK], BF16)

        x_codes = sbuf("x_codes", [P, PACK, G * R], U32)
        x_scales = sbuf("x_scales", [P, PACK, G * R], U8)
        w_codes = sbuf("w_codes", [P, 2, C], U32)
        w_scales = sbuf("w_scales", [P, 2, C], U8)
        ad_codes = sbuf("ad_codes", [P, J], U32)
        ad_scales = sbuf("ad_scales", [P, J], U8)
        h_codes = sbuf("h_codes", [P, CHUNKS, C], U32)
        h_scales = sbuf("h_scales", [P, CHUNKS, C], U8)
        y_codes = sbuf("y_codes", [P, N], U32)
        y_scales = sbuf("y_scales", [P, N], U8)

        sums = [sbuf("sums%d" % g, [P, N], F32) for g in range(G)]
        rounded = [[sbuf("rounded%d_%d" % (h, g), [P, H], BF16) for g in range(G)] for h in range(2)]
        y_out = [sbuf("y_out%d" % g, [P, N], F32) for g in range(G)]
        grouped = [sbuf("grouped%d" % h, [P, PACK, H], BF16) for h in range(2)]
        y_bf = [sbuf("y_bf%d" % h, [P, H, PACK], BF16) for h in range(2)]

        bank_a = [ps.tile([P, PACK, C], F32, name="bank_a%d" % r) for r in range(G)]
        bank_b = [ps.tile([P, PACK, C], F32, name="bank_b%d" % r) for r in range(G)]

        x_fill = x_raw[1][rows(1)].rearrange("p g j i -> p (g j i)")
        fill_cut = 2 * PACK * I - SCALAR_FILL
        nc.gpsimd.memset(zeros[rows(1)], 0.0)
        nc.vector.memset(w_raw[rows(1)].bitcast(I32), 0)
        nc.vector.memset(x_raw[0][rows(1)].bitcast(I32), 0)
        nc.gpsimd.memset(x_fill[:, :fill_cut].bitcast(I32), 0)

        tile_queue = [nc.sync, nc.scalar]
        w_rows = w.rearrange("(p j) (s b n) -> b p (j s) n", j=PACK, s=2, b=2)
        x_rows = x.rearrange("(m g) (p j) i -> m p g (j i)", m=2, j=PACK)
        for b in range(2):
            tile_queue[b].dma_start(out=w_raw[rows(2 * b)].rearrange("p j s n -> p (j s) n"), in_=w_rows[b])
        for m in range(2):
            for b in range(2):
                tile_queue[b].dma_start(out=x_raw[m][rows(2 * b)].rearrange("p g j i -> p g (j i)"), in_=x_rows[m])
        nc.sync.dma_start(out=ni_sb[:], in_=ni.rearrange("g (p t) o -> (g p) (t o)", t=PACK))
        bn_step = P // BN_COPIES
        nc.scalar.dma_start(out=bn_few[0:P:bn_step, :], in_=bn[0, :].partition_broadcast(BN_COPIES))
        nc.sync.dma_start(
            out=ad_raw[:].rearrange("p t j -> p (t j)"),
            in_=ad.rearrange("g (p t) j -> (g p) (t j)", t=PACK),
        )
        nc.scalar.activation(out=x_fill[:, fill_cut:], in_=zeros[rows(1)], func=ACT.Relu)
        nc.sync.dma_start(
            out=bn_all[:], in_=bn_few[0:P:bn_step, :].unsqueeze(1).to_broadcast([BN_COPIES, bn_step, N])
        )

        nc.vector.tensor_copy(
            out=w_bf[0:SPAN].rearrange("p s (c i) j -> p (s c) j i", i=RUN),
            in_=w_raw[0:SPAN].rearrange("p j s (c i) -> p (s c) j i", i=RUN),
        )
        x_dst = x_bf[0:SPAN].rearrange("p (a b) g q j -> p g a q j b", b=2)
        x_src = [x_raw[m][0:SPAN].rearrange("p g j (q a b) -> p g a q j b", a=2, b=2) for m in range(2)]

        def quantize_w(s):
            quantize(w_codes[0:SPAN, s, :], w_scales[0:SPAN, s, :], w_bf[0:SPAN, s].rearrange("p c j -> p (c j)"))

        nc.vector.tensor_copy(out=x_dst[:, 0], in_=x_src[0][:, 0])
        nc.scalar.copy(out=x_dst[:, 1], in_=x_src[0][:, 1])
        quantize_w(0)
        nc.vector.tensor_copy(out=x_dst[:, 2:4, 0], in_=x_src[1][:, :, 0])
        nc.scalar.copy(out=x_dst[:, 2:4, 1], in_=x_src[1][:, :, 1])
        quantize_w(1)
        nc.scalar.copy(
            out=ad_bf[:].rearrange("p (c i) t -> p c t i", i=RUN),
            in_=ad_raw[:].rearrange("p t (c i) -> p c t i", i=RUN),
        )

        def z_bank(chunk):
            s, b = divmod(chunk, 2)
            return (bank_a, bank_b)[s][2 * b]

        def first_product(t, chunk):
            s, b = divmod(chunk, 2)
            nc.tensor.matmul_mx(
                out=z_bank(chunk)[:, t, :],
                lhsT=x_codes[rows(2 * b), t, :].bitcast(FP8X4),
                lhsT_scale=x_scales[rows(2 * b), t, :],
                rhs=w_codes[rows(2 * b), s, :].bitcast(FP8X4),
                rhs_scale=w_scales[rows(2 * b), s, :],
                start=True,
                stop=True,
            )

        for t in range(PACK):
            quantize(x_codes[0:SPAN, t, :], x_scales[0:SPAN, t, :], x_bf[0:SPAN, t].rearrange("p g q j -> p (g q j)"))
            first_product(t, 1)
            first_product(t, 2)
        for chunk in (0, 3):
            for t in range(PACK):
                first_product(t, chunk)

        def scale_on_vector(chunk):
            nc.vector.tensor_tensor(
                out=h_bf[:, chunk].rearrange("p (c i) t -> p c t i", i=2),
                in0=z_bank(chunk)[:].rearrange("p t (c i) -> p c t i", i=2),
                in1=ni_sb[:].unsqueeze(1).unsqueeze(3).to_broadcast([P, C // 2, PACK, 2]),
                op=ALU.mult,
            )

        def scale_on_scalar(chunk):
            for t in range(PACK):
                nc.scalar.activation(
                    out=h_bf[:, chunk, :, t], in_=z_bank(chunk)[:, t, :], func=ACT.Copy, scale=ni_sb[:, t : t + 1]
                )

        def quantize_h(chunk):
            quantize(h_codes[:, chunk, :], h_scales[:, chunk, :], h_bf[:, chunk].rearrange("p c t -> p (c t)"))

        def y_bank(g, h):
            return (bank_a, bank_b)[h][g][:, 0:2, :]

        def second_product(chunks):
            for g in GRAPH_ORDER:
                for chunk in chunks:
                    nc.tensor.matmul_mx(
                        out=y_bank(g, chunk // 2)[:, chunk % 2, :],
                        lhsT=ad_codes[rows(g), :].bitcast(FP8X4),
                        lhsT_scale=ad_scales[rows(g), :],
                        rhs=h_codes[rows(g), chunk, :].bitcast(FP8X4),
                        rhs_scale=h_scales[rows(g), chunk, :],
                        start=True,
                        stop=True,
                    )

        def add_bias(dst, g, h):
            nc.vector.tensor_tensor(
                out=dst,
                in0=y_bank(g, h).rearrange("p r c -> p (r c)"),
                in1=bn_all[:, half_columns(h)],
                op=ALU.add,
            )

        def regroup(g, h):
            nc.sync.dma_start(out=grouped[h][rows(g)], in_=rounded[h][g][:])

        def add_round_regroup(g, h):
            add_bias(sums[g][:, half_columns(h)], g, h)
            nc.scalar.copy(out=rounded[h][g][:], in_=sums[g][:, half_columns(h)])
            regroup(g, h)

        scale_on_scalar(2)
        scale_on_vector(1)
        scale_on_vector(0)
        quantize(ad_codes[:], ad_scales[:], ad_bf[:].rearrange("p j t -> p (j t)"))
        quantize_h(1)
        quantize_h(0)
        second_product((1, 0))
        scale_on_vector(3)

        add_round_regroup(GRAPH_ORDER[0], 0)
        quantize_h(2)
        quantize_h(3)
        second_product((2, 3))
        for g in GRAPH_ORDER[1:]:
            add_round_regroup(g, 0)

        early, late = GRAPH_ORDER[:2], GRAPH_ORDER[2:]
        for g in early:
            add_round_regroup(g, 1)
        for g in late:
            add_bias(rounded[1][g][:], g, 1)
            regroup(g, 1)
        for g in late:
            add_bias(sums[g][:, half_columns(1)], g, 1)
        for g_early, g_late in zip(early, late):
            nc.scalar.activation(out=y_out[g_early][:], in_=sums[g_early][:], func=ACT.Relu)
            nc.sync.dma_start(out=out_0[J * g_early : J * g_early + J, :], in_=y_out[g_early][:])
            nc.vector.tensor_scalar(
                out=y_out[g_late][:], in0=sums[g_late][:], scalar1=0.0, scalar2=None, op0=ALU.max
            )
            nc.sync.dma_start(out=out_0[J * g_late : J * g_late + J, :], in_=y_out[g_late][:])

        cut = VECTOR_COLUMNS // RUN
        for h in range(2):
            dst = y_bf[h][:].rearrange("p (c i) u -> p c u i", i=RUN)
            src = grouped[h][:].rearrange("p u (c i) -> p c u i", i=RUN)
            nc.vector.tensor_scalar(out=dst[:, :cut], in0=src[:, :cut], scalar1=0.0, scalar2=None, op0=ALU.max)
            nc.scalar.activation(out=dst[:, cut:], in_=src[:, cut:], func=ACT.Relu)

        words = out_1.rearrange("s p n u -> (s p) (n u)").bitcast(I32)
        scale_rows = out_2.rearrange("s f n -> (s f) n").bitcast(I32)
        for h in range(2):
            cols = half_columns(h)
            quantize(y_codes[:, cols], y_scales[:, cols], y_bf[h][:].rearrange("p n u -> p (n u)"))
            nc.scalar.dma_start(out=words[:, cols], in_=y_codes[:, cols].bitcast(I32))
        blocks = J // 32
        for g in range(G):
            tile_queue[g // 2].dma_start(
                out=scale_rows[blocks * g : blocks * g + blocks, :],
                in_=y_scales[R * g : R * g + blocks, :].bitcast(I32),
            )
